import numpy as np
import ml_dtypes

BF16 = ml_dtypes.bfloat16


def bf(x):
    return np.asarray(x, np.float32).astype(BF16)


def f32(x):
    return np.asarray(x, np.float32)


def f64(x):
    return np.asarray(x).astype(np.float64)


def striped(idx):
    return np.concatenate([l.reshape(-1, 16).T for l in idx])


def rows(idx, k):
    return np.tile(np.repeat(idx, 16, axis=0), (k // (16 * 8), 1))


def look(tab, idx):
    return np.take_along_axis(f64(tab), rows(idx, len(tab)), axis=1)


K, S, V, N, M = 256, 2048, 2048, 2048, 256


def silu(v):
    return v / (1.0 + np.exp(-v))


def setup_inputs():
    return {"tab": f32(np.random.standard_normal((2, K, S))), "y": f32(np.random.standard_normal((K, V))), "w": bf(np.random.standard_normal((K, M)) / np.sqrt(K)), "b": f32(0.5 * np.random.standard_normal((M, 1))), "offs": striped(np.stack([np.random.permutation(S)[:N] for _ in range(8)]))}


def reference(tab, y, w, b, offs):
    idx = np.stack([g.T.reshape(-1) for g in np.split(offs, 8)])
    x = (np.minimum(look(tab[0], idx), f64(y))) * (silu(look(tab[1], idx)))
    return np.maximum(f64(w).T @ x + f64(b), 0.0)

@@ -1,0 +1,71 @@
+import concourse.mybir as mybir
+
+F32, BF16, U16 = mybir.dt.float32, mybir.dt.bfloat16, mybir.dt.uint16
+minimum, mult = mybir.AluOpType.min, mybir.AluOpType.mult
+silu, relu = mybir.ActivationFunctionType.Silu, mybir.ActivationFunctionType.Relu
+
+P = 128
+PIECE = 512
+ENTRIES_PER_COLUMN = 16
+
+FLOPS = 2 * 256 * 256 * 2048
+
+
+def tile_lookup_vg_minsilu_relu_kernel(tc, tab, y, w, b, offs, out):
+    nc = tc.nc
+    rows, columns = tab.shape[1], tab.shape[2]
+    outputs, entries = out.shape
+    row_blocks, output_blocks, pieces = rows // P, outputs // P, entries // PIECE
+    list_columns = PIECE // ENTRIES_PER_COLUMN
+
+    with (
+        tc.tile_pool(name="held", bufs=1) as held,
+        tc.tile_pool(name="work", bufs=row_blocks * pieces) as work,
+        tc.psum_pool(name="psum", bufs=1) as psum,
+    ):
+        lists = held.tile([P, entries // ENTRIES_PER_COLUMN], U16, name="lists")
+        nc.sync.dma_start(lists[:], offs)
+        gates, values, stream = [], [], []
+        for r in range(row_blocks):
+            block = slice(r * P, (r + 1) * P)
+            gates.append(held.tile([P, columns], F32, name=f"gates{r}"))
+            values.append(held.tile([P, columns], F32, name=f"values{r}"))
+            stream.append(held.tile([P, entries], F32, name=f"stream{r}"))
+            nc.sync.dma_start(gates[r][:], tab[1, block, :])
+            nc.sync.dma_start(values[r][:], tab[0, block, :])
+            nc.sync.dma_start(stream[r][:], y[block, :])
+
+        weights, bias = [], []
+        for r in range(row_blocks):
+            weights.append(held.tile([P, outputs], BF16, name=f"weights{r}"))
+            nc.gpsimd.dma_start(weights[r][:], w[r * P : (r + 1) * P, :])
+        for m in range(output_blocks):
+            bias.append(held.tile([P, 1], F32, name=f"bias{m}"))
+            nc.gpsimd.dma_start(bias[m][:], b[m * P : (m + 1) * P, :])
+
+        banks = [
+            [psum.tile([P, PIECE], F32, name=f"bank{m}_{j}") for j in range(pieces)]
+            for m in range(output_blocks)
+        ]
+
+        for r in range(row_blocks):
+            for j in range(pieces):
+                part = slice(j * PIECE, (j + 1) * PIECE)
+                picked = lists[:, j * list_columns : (j + 1) * list_columns]
+
+                gate = work.tile([P, PIECE], F32, name="gate")
+                nc.scalar.activation(gate[:], gates[r][:].indirect(picked), silu)
+                value = work.tile([P, PIECE], F32, name="value")
+                nc.vector.tensor_tensor(value[:], values[r][:].indirect(picked), stream[r][:, part], minimum)
+                x = work.tile([P, PIECE], BF16, name="x")
+                nc.vector.tensor_tensor(x[:], value[:], gate[:], mult)
+
+                for m in range(output_blocks):
+                    nc.tensor.matmul(
+                        banks[m][j][:], weights[r][:, m * P : (m + 1) * P], x[:],
+                        start=(r == 0), stop=(r == row_blocks - 1),
+                    )
+                    if r == row_blocks - 1:
+                        result = work.tile([P, PIECE], F32, name="result")
+                        nc.scalar.activation(result[:], banks[m][j][:], relu, bias=bias[m][:])
+                        nc.sync.dma_start(out[m * P : (m + 1) * P, part], result[:])

@@ -25,20 +25,20 @@ def tile_lookup_vg_minsilu_relu_kernel(tc, tab, y, w, b, offs, out):
     ):
         lists = held.tile([P, entries // ENTRIES_PER_COLUMN], U16, name="lists")
         nc.sync.dma_start(lists[:], offs)
-        gates, values, stream = [], [], []
+        gates, values, stream, weights = [], [], [], []
         for r in range(row_blocks):
             block = slice(r * P, (r + 1) * P)
             gates.append(held.tile([P, columns], F32, name=f"gates{r}"))
             values.append(held.tile([P, columns], F32, name=f"values{r}"))
-            stream.append(held.tile([P, entries], F32, name=f"stream{r}"))
             nc.sync.dma_start(gates[r][:], tab[1, block, :])
             nc.sync.dma_start(values[r][:], tab[0, block, :])
-            nc.sync.dma_start(stream[r][:], y[block, :])
-
-        weights, bias = [], []
-        for r in range(row_blocks):
+            stream.append([held.tile([P, PIECE], F32, name=f"stream{r}_{j}") for j in range(pieces)])
+            for j in range(pieces):
+                nc.sync.dma_start(stream[r][j][:], y[block, j * PIECE : (j + 1) * PIECE])
             weights.append(held.tile([P, outputs], BF16, name=f"weights{r}"))
-            nc.gpsimd.dma_start(weights[r][:], w[r * P : (r + 1) * P, :])
+            nc.sync.dma_start(weights[r][:], w[block, :])
+
+        bias = []
         for m in range(output_blocks):
             bias.append(held.tile([P, 1], F32, name=f"bias{m}"))
             nc.gpsimd.dma_start(bias[m][:], b[m * P : (m + 1) * P, :])
@@ -56,7 +56,7 @@ def tile_lookup_vg_minsilu_relu_kernel(tc, tab, y, w, b, offs, out):
                 gate = work.tile([P, PIECE], F32, name="gate")
                 nc.scalar.activation(gate[:], gates[r][:].indirect(picked), silu)
                 value = work.tile([P, PIECE], F32, name="value")
-                nc.vector.tensor_tensor(value[:], values[r][:].indirect(picked), stream[r][:, part], minimum)
+                nc.vector.tensor_tensor(value[:], values[r][:].indirect(picked), stream[r][j][:], minimum)
                 x = work.tile([P, PIECE], BF16, name="x")
                 nc.vector.tensor_tensor(x[:], value[:], gate[:], mult)
 

@@ -38,10 +38,9 @@ def tile_lookup_vg_minsilu_relu_kernel(tc, tab, y, w, b, offs, out):
             weights.append(held.tile([P, outputs], BF16, name=f"weights{r}"))
             nc.sync.dma_start(weights[r][:], w[block, :])
 
-        bias = []
-        for m in range(output_blocks):
-            bias.append(held.tile([P, 1], F32, name=f"bias{m}"))
-            nc.gpsimd.dma_start(bias[m][:], b[m * P : (m + 1) * P, :])
+        bias = held.tile([P, output_blocks], F32, name="bias")
+        with nc.allow_non_contiguous_dma(reason="256 single values, loaded once"):
+            nc.sync.dma_start(bias[:], b.rearrange("(m p) one -> p (m one)", p=P))
 
         banks = [
             [psum.tile([P, PIECE], F32, name=f"bank{m}_{j}") for j in range(pieces)]
@@ -67,5 +66,5 @@ def tile_lookup_vg_minsilu_relu_kernel(tc, tab, y, w, b, offs, out):
                     )
                     if r == row_blocks - 1:
                         result = work.tile([P, PIECE], F32, name="result")
-                        nc.scalar.activation(result[:], banks[m][j][:], relu, bias=bias[m][:])
+                        nc.scalar.activation(result[:], banks[m][j][:], relu, bias=bias[:, m : m + 1])
                         nc.sync.dma_start(out[m * P : (m + 1) * P, part], result[:])

import concourse.mybir as mybir

F32, BF16, U16 = mybir.dt.float32, mybir.dt.bfloat16, mybir.dt.uint16
minimum, mult = mybir.AluOpType.min, mybir.AluOpType.mult
silu, relu = mybir.ActivationFunctionType.Silu, mybir.ActivationFunctionType.Relu

P = 128
PIECE = 512
ENTRIES_PER_COLUMN = 16

FLOPS = 2 * 256 * 256 * 2048


def tile_lookup_vg_minsilu_relu_kernel(tc, tab, y, w, b, offs, out):
    nc = tc.nc
    rows, columns = tab.shape[1], tab.shape[2]
    outputs, entries = out.shape
    row_blocks, output_blocks, pieces = rows // P, outputs // P, entries // PIECE
    list_columns = PIECE // ENTRIES_PER_COLUMN

    with (
        tc.tile_pool(name="held", bufs=1) as held,
        tc.tile_pool(name="work", bufs=row_blocks * pieces) as work,
        tc.psum_pool(name="psum", bufs=1) as psum,
    ):
        lists = held.tile([P, entries // ENTRIES_PER_COLUMN], U16, name="lists")
        nc.sync.dma_start(lists[:], offs)
        gates, values, stream, weights = [], [], [], []
        for r in range(row_blocks):
            block = slice(r * P, (r + 1) * P)
            gates.append(held.tile([P, columns], F32, name=f"gates{r}"))
            values.append(held.tile([P, columns], F32, name=f"values{r}"))
            nc.sync.dma_start(gates[r][:], tab[1, block, :])
            nc.sync.dma_start(values[r][:], tab[0, block, :])
            stream.append([held.tile([P, PIECE], F32, name=f"stream{r}_{j}") for j in range(pieces)])
            for j in range(pieces):
                nc.sync.dma_start(stream[r][j][:], y[block, j * PIECE : (j + 1) * PIECE])
            weights.append(held.tile([P, outputs], BF16, name=f"weights{r}"))
            nc.sync.dma_start(weights[r][:], w[block, :])

        bias = held.tile([P, output_blocks], F32, name="bias")
        with nc.allow_non_contiguous_dma(reason="256 single values, loaded once"):
            nc.sync.dma_start(bias[:], b.rearrange("(m p) one -> p (m one)", p=P))

        banks = [
            [psum.tile([P, PIECE], F32, name=f"bank{m}_{j}") for j in range(pieces)]
            for m in range(output_blocks)
        ]

        for r in range(row_blocks):
            for j in range(pieces):
                part = slice(j * PIECE, (j + 1) * PIECE)
                picked = lists[:, j * list_columns : (j + 1) * list_columns]

                gate = work.tile([P, PIECE], F32, name="gate")
                nc.scalar.activation(gate[:], gates[r][:].indirect(picked), silu)
                value = work.tile([P, PIECE], F32, name="value")
                nc.vector.tensor_tensor(value[:], values[r][:].indirect(picked), stream[r][j][:], minimum)
                x = work.tile([P, PIECE], BF16, name="x")
                nc.vector.tensor_tensor(x[:], value[:], gate[:], mult)

                for m in range(output_blocks):
                    nc.tensor.matmul(
                        banks[m][j][:], weights[r][:, m * P : (m + 1) * P], x[:],
                        start=(r == 0), stop=(r == row_blocks - 1),
                    )
                    if r == row_blocks - 1:
                        result = work.tile([P, PIECE], F32, name="result")
                        nc.scalar.activation(result[:], banks[m][j][:], relu, bias=bias[:, m : m + 1])
                        nc.sync.dma_start(out[m * P : (m + 1) * P, part], result[:])
